import numpy as np
import ml_dtypes


def mxq(x, axis, fmt="e4m3"):
    dtype, down = {"e4m3": (ml_dtypes.float8_e4m3fn, 7), "e5m2": (ml_dtypes.float8_e5m2, 14)}[fmt]
    v = np.moveaxis(np.asarray(x, np.float32).astype(ml_dtypes.bfloat16).astype(np.float64), axis, -1)
    blocks = v.reshape(v.shape[:-1] + (-1, 32))
    amax = np.abs(blocks).max(-1, keepdims=True)
    byte = np.maximum(np.where(amax > 0, np.frexp(amax)[1] - 1 + 127, 0) - down, 1)
    scale = np.exp2(byte - 127.0)
    codes = (blocks / scale).astype(np.float32).astype(dtype).astype(np.float64)
    return np.moveaxis((codes * scale).reshape(v.shape), -1, axis)


WIDE = False


def mx_kscale(k):
    if not WIDE:
        return np.ones(k)
    levels = np.array([10, -10, 5, -5, 0])
    if k % 512:
        return np.exp2(np.random.permutation(np.resize(levels, k // 32))).repeat(32)
    a = np.empty((k // 512, 16))
    for p in range(k // 512):
        a[p, :8] = np.random.permutation(np.resize(levels, 8))
        for g in range(8):
            far = levels[np.abs(levels - a[p, g]) >= 10]
            a[p, g + 8] = far[np.random.randint(len(far))]
    return np.exp2(a.ravel()).repeat(32)


def f64(x):
    return np.asarray(x).astype(np.float64)


def striped(idx):
    return np.tile(np.asarray(idx).reshape(-1, 16).T, (8, 1)).astype(np.uint16)


def unstriped(offs):
    return offs[:16].T.reshape(-1).astype(np.int64)


E2M1 = np.array([0.0, 0.5, 1.0, 1.5, 2.0, 3.0, 4.0, 6.0, -0.0, -0.5, -1.0, -1.5, -2.0, -3.0, -4.0, -6.0])


def pack_weight(w, fmt):
    k, n = w.shape
    w = f64(np.asarray(w, np.float32).astype(ml_dtypes.bfloat16)).reshape(k // 32, 32, n)
    amax = np.abs(w).max(1)
    if fmt == "e4m3":
        byte = np.frexp(amax)[1] - 1 + 127 - 7
    else:
        mant, ex = np.frexp(amax / 6.0)
        byte = np.where(mant > 0.5, ex, ex - 1) + 127
    byte = np.clip(np.where(amax > 0, byte, 1), 1, 254)
    scaled = (w * np.exp2(127.0 - byte)[:, None, :]).reshape(k, n).astype(np.float32)
    by_word = np.ascontiguousarray(scaled.reshape(k // 512, 128, 4, n).transpose(0, 1, 3, 2))
    if fmt == "e4m3":
        words = by_word.astype(ml_dtypes.float8_e4m3fn).view(np.uint8)
    else:
        c = by_word.astype(ml_dtypes.float4_e2m1fn).view(np.uint8) & 0xF
        words = (c[..., 0::2] | (c[..., 1::2] << 4)).reshape(k // 512, 128, 2 * n)
    return np.ascontiguousarray(words), np.ascontiguousarray(byte.astype(np.uint8).reshape(k // 512, 16, n))


def unpack_weight(words, scales, fmt):
    g, _, n = scales.shape
    words = np.ascontiguousarray(words).reshape(g, 128, n, -1)
    if fmt == "e4m3":
        vals = words.view(ml_dtypes.float8_e4m3fn).astype(np.float64)
    else:
        nib = np.empty((g, 128, n, 4), np.uint8)
        nib[..., 0::2] = words & 0xF
        nib[..., 1::2] = words >> 4
        vals = E2M1[nib]
    vals = vals * np.repeat(np.exp2(scales.astype(np.float64) - 127.0), 8, axis=1)[..., None]
    return vals.transpose(0, 1, 3, 2).reshape(g * 512, n)


D, T, I, Q, E = 512, 2048, 512, 128, 512


def setup_inputs():
    n = np.random.standard_normal
    idx = np.random.permutation(T)[:I]
    fd = mx_kscale(D)
    fi = mx_kscale(I)
    ti = np.ones(T)
    ti[idx] = fi
    keysp = pack_weight(n((D, T)) / fd[:, None], "e2m1")
    return {
        "query": (n((D, Q)) * 0.7 / np.sqrt(D) * fd[:, None]).astype(np.float32),
        "query2": (n((D, Q)) * 0.7 / np.sqrt(D) * fd[:, None]).astype(np.float32),
        "keys_words": keysp[0],
        "keys_scales": keysp[1],
        "xmark": np.tile(np.random.uniform(-1.0, 1.0, T), (128, 1)).astype(np.float32),
        "ymark": np.tile(np.random.uniform(-1.0, 1.0, T), (128, 1)).astype(np.float32),
        "lam": (np.random.uniform(0.5, 1.2, (Q, 1))).astype(np.float32),
        "lean": (np.random.uniform(0.2, 0.6, (Q, 1))).astype(np.float32),
        "os": (np.random.uniform(4.0, 16.0, (1, I)) * fi).astype(np.float32),
        "vals": (n((E, T)) / ti).astype(np.float32),
        "vsharp": (np.random.uniform(0.6, 1.2, (Q, 1))).astype(np.float32),
        "offs": striped(idx),
    }


def reference(query, query2, keys_words, keys_scales, xmark, ymark, lam, lean, os, vals, vsharp, offs):
    idx = unstriped(offs)
    keysu = unpack_weight(keys_words, keys_scales, "e2m1")
    queryq = mxq(f64(query), 0, "e4m3")
    keysidxg = keysu[:, idx]
    a = queryq.T @ keysidxg
    query2q = mxq(f64(query2), 0, "e4m3")
    b = query2q.T @ keysidxg
    dx = a - f64(xmark)[:1][:, idx]
    dy = b - f64(ymark)[:1][:, idx]
    s = (np.square(dx) + np.square(dy)) * f64(lam) * (-1.0)
    p = np.exp(s - np.max(s, axis=1, keepdims=True))
    r = p / np.sum(p, axis=1, keepdims=True)
    m0 = np.sum(r * s, axis=1, keepdims=True)
    w = r * ((s - m0) * f64(lean) + 1.0)
    wo1 = w * f64(os)
    wt1 = wo1.T
    vt1 = f64(vals)[:, idx].T
    wt1q = mxq(wt1, 0, "e4m3")
    vt1q = mxq(vt1, 0, "e4m3")
    o = wt1q.T @ vt1q
    oz = o * f64(vsharp)
    oe = np.exp(oz - np.max(oz, axis=1, keepdims=True))
    y = oe / np.sum(oe, axis=1, keepdims=True) * 512.0
    return y

@@ -1,0 +1,236 @@
+from contextlib import ExitStack
+
+import concourse.mybir as mybir
+from concourse.masks import make_identity
+
+D, T, I, Q, E = 512, 2048, 512, 128, 512
+P = 128
+PACK = 4
+FLOPS = 2 * D * Q * I * 2 + 2 * I * Q * E
+BYTES = 2 * D * Q * 4 + P * 2 * T + 16 * T + 2 * T * 4 + 3 * Q * 4 + I * 4 + E * T * 4 + P * 64 + Q * E * 4
+
+F32 = mybir.dt.float32
+BF16 = mybir.dt.bfloat16
+I32 = mybir.dt.int32
+U32 = mybir.dt.uint32
+U16 = mybir.dt.uint16
+U8 = mybir.dt.uint8
+FP8X4 = mybir.dt.float8_e4m3fn_x4
+FP4X4 = mybir.dt.float4_e2m1fn_x4
+ALU = mybir.AluOpType
+ACT = mybir.ActivationFunctionType
+MARK_ROW = P - 1
+
+
+def tile_attend_maplace_leaning_readshares_kernel(
+    tc, query, query2, keys_words, keys_scales, xmark, ymark, lam, lean, slot_factor, vals, vsharp, offs, out
+):
+    nc = tc.nc
+    with ExitStack() as ctx:
+        sb = ctx.enter_context(tc.tile_pool(name="sb", bufs=1))
+        ps = ctx.enter_context(tc.psum_pool(name="ps", bufs=1))
+        ps2 = ctx.enter_context(tc.psum_pool(name="ps2", bufs=2))
+
+        offsets = sb.tile([P, I // 16], U16, name="offsets")
+        nc.sync.dma_start(offsets[:], offs)
+
+        kscale_pool = sb.tile([P, T], U8, name="kscale_pool", align_bytes=64)
+        nc.vector.memset(kscale_pool[:].bitcast(I32), 0)
+        for quad in range(4):
+            nc.scalar.dma_start(
+                kscale_pool[32 * quad : 32 * quad + 4, :].bitcast(I32),
+                keys_scales[0, 4 * quad : 4 * quad + 4, :].bitcast(I32),
+            )
+        mark_pools = []
+        for name, mark in (("xpool", xmark), ("ypool", ymark)):
+            mark_pool = sb.tile([P, T], F32, name=name, align_bytes=64)
+            nc.sync.dma_start(mark_pool[MARK_ROW:P, :], mark[MARK_ROW:P, :])
+            mark_pools.append(mark_pool)
+        nc.vector.memset(mark_pools[0][0:MARK_ROW, :], 0.0)
+        kword_pool = sb.tile([P, T], U16, name="kword_pool", align_bytes=64)
+        nc.sync.dma_start(kword_pool[:].bitcast(I32), keys_words[0].bitcast(I32))
+        q_raw = []
+        for name, src in (("q_raw0", query), ("q_raw1", query2)):
+            raw = sb.tile([P, PACK, Q], F32, name=name, align_bytes=64)
+            nc.sync.dma_start(raw[:], src.rearrange("(p j) w -> p j w", j=PACK))
+            q_raw.append(raw)
+        val_pools = []
+        for j in range(4):
+            val_pool = sb.tile([P, T], F32, name="val_pool%d" % j, align_bytes=64)
+            nc.sync.dma_start(val_pool[:], vals[j * P : (j + 1) * P, :])
+            val_pools.append(val_pool)
+
+        ident = sb.tile([P, P], F32, name="ident", align_bytes=64)
+        make_identity(nc, ident[:])
+        warm = sb.tile([P, 1], F32, name="warm")
+        nc.scalar.activation(warm[:], ident[:, 0:1], ACT.Exp)
+
+        lam_col = sb.tile([P, 1], F32, name="lam_col")
+        nc.gpsimd.dma_start(lam_col[:], lam)
+        nc.gpsimd.memset(mark_pools[1][0:MARK_ROW, :], 0.0)
+        lean_col = sb.tile([P, 1], F32, name="lean_col")
+        nc.gpsimd.dma_start(lean_col[:], lean)
+        os_cols = sb.tile([P, PACK], F32, name="os_cols")
+        nc.gpsimd.dma_start(os_cols[:], slot_factor.rearrange("o (p t) -> (o p) t", t=PACK))
+        vs_col = sb.tile([P, 1], F32, name="vs_col")
+        nc.gpsimd.dma_start(vs_col[:], vsharp)
+        nvs_col = sb.tile([P, 1], F32, name="nvs_col")
+        nc.gpsimd.tensor_scalar(nvs_col[:], vs_col[:], -1.0, 0.0, ALU.mult, ALU.add)
+
+        mark_cols = []
+
+        def mark_columns(m):
+            picked = sb.tile([P, I], F32, name="mark_picked%d" % m, align_bytes=64)
+            nc.vector.tensor_copy(picked[:], mark_pools[m][:].indirect(offsets[:]))
+            turned = ps.tile([P, 4, P], F32, name="mark_turned%d" % m, tag="bank_m%d" % m)
+            for r in range(4):
+                nc.tensor.transpose(turned[:, r, :], picked[:, r * P : (r + 1) * P], ident[:])
+            cols = sb.tile([P, 4], F32, name="mark_cols%d" % m)
+            nc.scalar.copy(cols[:], turned[:, :, MARK_ROW])
+            mark_cols.append(cols)
+
+        mark_columns(0)
+
+        q_grouped = sb.tile([P, 2 * Q, PACK], BF16, name="q_grouped", align_bytes=64)
+        for m in range(2):
+            nc.scalar.copy(q_grouped[:, m * Q : (m + 1) * Q, :], q_raw[m][:].rearrange("p j w -> p w j"))
+
+        kscales = sb.tile([P, I], U8, name="kscales", align_bytes=64)
+        nc.vector.tensor_copy(kscales[:], kscale_pool[:].indirect(offsets[:]))
+        mark_columns(1)
+        q_codes = sb.tile([P, 2 * Q], U32, name="q_codes", align_bytes=64)
+        q_scales = sb.tile([P, 2 * Q], U8, name="q_scales", align_bytes=64)
+        nc.vector.quantize_mx(
+            out=q_codes[:].bitcast(FP8X4), scales=q_scales[:], in_=q_grouped[:].rearrange("p w j -> p (w j)")
+        )
+        kwords = sb.tile([P, I], U16, name="kwords", align_bytes=64)
+        points = []
+        for h in range(2):
+            nc.vector.tensor_copy(
+                kwords[:, h * 256 : (h + 1) * 256], kword_pool[:].indirect(offsets[:, h * 16 : (h + 1) * 16])
+            )
+            bank = ps.tile([P, 2, 2 * Q], F32, name="points%d" % h)
+            for c in range(2):
+                cols = slice((2 * h + c) * P, (2 * h + c + 1) * P)
+                nc.tensor.matmul_mx(
+                    out=bank[:, c, :],
+                    lhsT=kwords[:, cols].bitcast(FP4X4),
+                    lhsT_scale=kscales[:, cols],
+                    rhs=q_codes[:].bitcast(FP8X4),
+                    rhs_scale=q_scales[:],
+                    start=True,
+                    stop=True,
+                )
+            points.append(bank)
+
+        v_codes = sb.tile([P, E], U32, name="v_codes", align_bytes=64)
+        v_scales = sb.tile([P, E], U8, name="v_scales", align_bytes=64)
+        val_picked = []
+
+        def gather_values(j):
+            picked = sb.tile([P, I], BF16, name="val_picked%d" % j, align_bytes=64)
+            nc.vector.tensor_copy(picked[:], val_pools[j][:].indirect(offsets[:]))
+            val_picked.append(picked)
+
+        def quantize_values(j):
+            pairs = val_picked[j][:].bitcast(F32)
+            turned = ps2.tile([P, 2, P], F32, name="val_turned")
+            for u in range(2):
+                nc.tensor.transpose(turned[:, u, :], pairs[:, u : 2 * P : 2], ident[:])
+            grouped = sb.tile([P, P * PACK], BF16, name="val_grouped%d" % j, align_bytes=64)
+            nc.scalar.copy(
+                grouped[:].bitcast(F32).rearrange("p (e u) -> p e u", u=2), turned[:].rearrange("p u e -> p e u")
+            )
+            nc.vector.quantize_mx(
+                out=v_codes[:, j * P : (j + 1) * P].bitcast(FP8X4),
+                scales=v_scales[:, j * P : (j + 1) * P],
+                in_=grouped[:],
+            )
+
+        gather_values(0)
+        gather_values(1)
+
+        dist = ps.tile([P, I], F32, name="dist")
+        for r in range(4):
+            sq = sb.tile([P, 2, Q], F32, name="sq%d" % r, align_bytes=64)
+            for m in range(2):
+                nc.scalar.activation(
+                    sq[:, m, :],
+                    points[r // 2][:, r % 2, m * Q : (m + 1) * Q],
+                    ACT.Square,
+                    bias=mark_cols[m][:, r : r + 1],
+                    scale=-1.0,
+                )
+            for m in range(2):
+                nc.tensor.matmul(
+                    dist[:, r * P : (r + 1) * P],
+                    lhsT=sq[:, m, :],
+                    rhs=ident[:],
+                    is_transpose=True,
+                    start=(m == 0),
+                    stop=(m == 1),
+                )
+
+        ns = sb.tile([P, PACK, P], F32, name="ns", tag="val_pool1", align_bytes=64)
+        ns_min = sb.tile([P, 1], F32, name="ns_min")
+        nc.vector.tensor_scalar(
+            ns[:], dist[:].rearrange("q (s t) -> q t s", t=PACK), lam_col[:], None, ALU.mult, ALU.min,
+            accum_out=ns_min[:],
+        )
+        ns_flat = ns[:].rearrange("q t s -> q (t s)")
+        share = sb.tile([P, I], F32, name="share", align_bytes=64)
+        total = sb.tile([P, 1], F32, name="total")
+        nc.scalar.activation(share[:], ns_flat, ACT.Exp, bias=ns_min[:], scale=-1.0, accum_out=total[:])
+        gap = sb.tile([P, I], F32, name="gap", align_bytes=64)
+        nc.vector.tensor_scalar(gap[:], ns_flat, ns_min[:], lean_col[:], ALU.subtract, ALU.mult)
+        gather_values(2)
+        inv = sb.tile([P, 1], F32, name="inv")
+        nc.vector.reciprocal(inv[:], total[:])
+        pull = sb.tile([P, I], F32, name="pull", tag="val_pool2", align_bytes=64)
+        mean = sb.tile([P, 1], F32, name="mean")
+        nc.vector.scalar_tensor_tensor(pull[:], gap[:], inv[:], share[:], ALU.mult, ALU.mult, accum_out=mean[:])
+        coef = sb.tile([P, 1], F32, name="coef")
+        nc.vector.tensor_scalar(coef[:], mean[:], 1.0, inv[:], ALU.add, ALU.mult)
+        w = sb.tile([P, I], F32, name="w", align_bytes=64)
+        nc.vector.scalar_tensor_tensor(w[:], share[:], coef[:], pull[:], ALU.mult, ALU.subtract)
+        gather_values(3)
+        w_turned = ps.tile([P, PACK, Q], F32, name="w_turned", tag="bank_m1")
+        for t in range(PACK):
+            nc.tensor.transpose(w_turned[:, t, :], w[:, t * P : (t + 1) * P], ident[:])
+        w_grouped = sb.tile([P, Q, PACK], BF16, name="w_grouped", tag="val_pool3", align_bytes=64)
+        nc.vector.tensor_tensor(
+            w_grouped[:],
+            w_turned[:].rearrange("p t q -> p q t"),
+            os_cols[:].unsqueeze(1).to_broadcast([P, Q, PACK]),
+            ALU.mult,
+        )
+        w_codes = sb.tile([P, Q], U32, name="w_codes", align_bytes=64)
+        w_scales = sb.tile([P, Q], U8, name="w_scales", align_bytes=64)
+        nc.vector.quantize_mx(
+            out=w_codes[:].bitcast(FP8X4), scales=w_scales[:], in_=w_grouped[:].rearrange("p q t -> p (q t)")
+        )
+
+        for j in range(4):
+            quantize_values(j)
+
+        o = ps.tile([P, E], F32, name="o", tag="bank_m0")
+        nc.tensor.matmul_mx(
+            out=o[:],
+            lhsT=w_codes[:].bitcast(FP8X4),
+            lhsT_scale=w_scales[:],
+            rhs=v_codes[:].bitcast(FP8X4),
+            rhs_scale=v_scales[:],
+            start=True,
+            stop=True,
+        )
+        noz = sb.tile([P, E], F32, name="noz", align_bytes=64)
+        noz_min = sb.tile([P, 1], F32, name="noz_min")
+        nc.vector.tensor_scalar(noz[:], o[:], nvs_col[:], None, ALU.mult, ALU.min, accum_out=noz_min[:])
+        oe = sb.tile([P, E], F32, name="oe", align_bytes=64)
+        oe_sum = sb.tile([P, 1], F32, name="oe_sum")
+        nc.scalar.activation(oe[:], noz[:], ACT.Exp, bias=noz_min[:], scale=-1.0, accum_out=oe_sum[:])
+        oe_inv = sb.tile([P, 1], F32, name="oe_inv")
+        nc.vector.reciprocal(oe_inv[:], oe_sum[:])
+        y = sb.tile([P, E], F32, name="y", align_bytes=64)
+        nc.vector.tensor_scalar(y[:], oe[:], oe_inv[:], float(E), ALU.mult, ALU.mult)
+        nc.sync.dma_start(out, y[:])

@@ -20,6 +20,7 @@ FP4X4 = mybir.dt.float4_e2m1fn_x4
 ALU = mybir.AluOpType
 ACT = mybir.ActivationFunctionType
 MARK_ROW = P - 1
+X_SPLIT = 768
 
 
 def tile_attend_maplace_leaning_readshares_kernel(
@@ -29,24 +30,33 @@ def tile_attend_maplace_leaning_readshares_kernel(
     with ExitStack() as ctx:
         sb = ctx.enter_context(tc.tile_pool(name="sb", bufs=1))
         ps = ctx.enter_context(tc.psum_pool(name="ps", bufs=1))
-        ps2 = ctx.enter_context(tc.psum_pool(name="ps2", bufs=2))
 
         offsets = sb.tile([P, I // 16], U16, name="offsets")
         nc.sync.dma_start(offsets[:], offs)
 
+        def load_mark(name, mark):
+            mark_pool = sb.tile([P, T + 1], F32, name=name, align_bytes=64)
+            nc.sync.dma_start(mark_pool[MARK_ROW:P, 0:T], mark[MARK_ROW:P, :])
+            return mark_pool
+
+        def load_values(j):
+            val_pool = sb.tile([P, T], F32, name="val_pool%d" % j, align_bytes=64)
+            nc.sync.dma_start(val_pool[:], vals[j * P : (j + 1) * P, :])
+            return val_pool
+
+        def load_column(name, src):
+            col = sb.tile([P, 1], F32, name=name, align_bytes=64)
+            nc.sync.dma_start(col[:], src)
+            return col
+
+        mark_pools = [load_mark("xpool", xmark)]
         kscale_pool = sb.tile([P, T], U8, name="kscale_pool", align_bytes=64)
-        nc.vector.memset(kscale_pool[:].bitcast(I32), 0)
+        nc.gpsimd.memset(kscale_pool[:].bitcast(I32), 0)
         for quad in range(4):
-            nc.scalar.dma_start(
+            nc.sync.dma_start(
                 kscale_pool[32 * quad : 32 * quad + 4, :].bitcast(I32),
                 keys_scales[0, 4 * quad : 4 * quad + 4, :].bitcast(I32),
             )
-        mark_pools = []
-        for name, mark in (("xpool", xmark), ("ypool", ymark)):
-            mark_pool = sb.tile([P, T], F32, name=name, align_bytes=64)
-            nc.sync.dma_start(mark_pool[MARK_ROW:P, :], mark[MARK_ROW:P, :])
-            mark_pools.append(mark_pool)
-        nc.vector.memset(mark_pools[0][0:MARK_ROW, :], 0.0)
         kword_pool = sb.tile([P, T], U16, name="kword_pool", align_bytes=64)
         nc.sync.dma_start(kword_pool[:].bitcast(I32), keys_words[0].bitcast(I32))
         q_raw = []
@@ -54,60 +64,58 @@ def tile_attend_maplace_leaning_readshares_kernel(
             raw = sb.tile([P, PACK, Q], F32, name=name, align_bytes=64)
             nc.sync.dma_start(raw[:], src.rearrange("(p j) w -> p j w", j=PACK))
             q_raw.append(raw)
-        val_pools = []
-        for j in range(4):
-            val_pool = sb.tile([P, T], F32, name="val_pool%d" % j, align_bytes=64)
-            nc.sync.dma_start(val_pool[:], vals[j * P : (j + 1) * P, :])
-            val_pools.append(val_pool)
+        mark_pools.append(load_mark("ypool", ymark))
+        lam_col = load_column("lam_col", lam)
+        val_pools = [load_values(0)]
+        lean_col = load_column("lean_col", lean)
+        val_pools.extend([load_values(j) for j in range(1, 4)])
+        os_cols = sb.tile([P, PACK], F32, name="os_cols")
+        nc.sync.dma_start(os_cols[:], slot_factor.rearrange("o (p t) -> (o p) t", t=PACK))
+        vs_col = load_column("vs_col", vsharp)
 
+        warm_in = sb.tile([P, 1], F32, name="warm_in")
+        nc.gpsimd.memset(warm_in[:], 0.0)
+        warm = sb.tile([P, 1], F32, name="warm")
+        nc.scalar.activation(warm[:], warm_in[:], ACT.Exp)
         ident = sb.tile([P, P], F32, name="ident", align_bytes=64)
         make_identity(nc, ident[:])
-        warm = sb.tile([P, 1], F32, name="warm")
-        nc.scalar.activation(warm[:], ident[:, 0:1], ACT.Exp)
-
-        lam_col = sb.tile([P, 1], F32, name="lam_col")
-        nc.gpsimd.dma_start(lam_col[:], lam)
-        nc.gpsimd.memset(mark_pools[1][0:MARK_ROW, :], 0.0)
-        lean_col = sb.tile([P, 1], F32, name="lean_col")
-        nc.gpsimd.dma_start(lean_col[:], lean)
-        os_cols = sb.tile([P, PACK], F32, name="os_cols")
-        nc.gpsimd.dma_start(os_cols[:], slot_factor.rearrange("o (p t) -> (o p) t", t=PACK))
-        vs_col = sb.tile([P, 1], F32, name="vs_col")
-        nc.gpsimd.dma_start(vs_col[:], vsharp)
+        nc.gpsimd.memset(mark_pools[0][0:MARK_ROW, 0:X_SPLIT], 0.0)
+        nc.vector.memset(mark_pools[0][0:MARK_ROW, X_SPLIT : T + 1], 0.0)
+        nc.gpsimd.memset(mark_pools[1][0:MARK_ROW, 0:T], 0.0)
         nvs_col = sb.tile([P, 1], F32, name="nvs_col")
         nc.gpsimd.tensor_scalar(nvs_col[:], vs_col[:], -1.0, 0.0, ALU.mult, ALU.add)
 
         mark_cols = []
 
-        def mark_columns(m):
+        def mark_columns(m, tag):
             picked = sb.tile([P, I], F32, name="mark_picked%d" % m, align_bytes=64)
-            nc.vector.tensor_copy(picked[:], mark_pools[m][:].indirect(offsets[:]))
+            nc.vector.tensor_copy(picked[:], mark_pools[m][:, 0:T].indirect(offsets[:]))
             turned = ps.tile([P, 4, P], F32, name="mark_turned%d" % m, tag="bank_m%d" % m)
             for r in range(4):
                 nc.tensor.transpose(turned[:, r, :], picked[:, r * P : (r + 1) * P], ident[:])
-            cols = sb.tile([P, 4], F32, name="mark_cols%d" % m)
+            cols = sb.tile([P, 4], F32, name="mark_cols%d" % m, tag=tag, align_bytes=64)
             nc.scalar.copy(cols[:], turned[:, :, MARK_ROW])
             mark_cols.append(cols)
-
-        mark_columns(0)
 
         q_grouped = sb.tile([P, 2 * Q, PACK], BF16, name="q_grouped", align_bytes=64)
         for m in range(2):
             nc.scalar.copy(q_grouped[:, m * Q : (m + 1) * Q, :], q_raw[m][:].rearrange("p j w -> p w j"))
 
-        kscales = sb.tile([P, I], U8, name="kscales", align_bytes=64)
-        nc.vector.tensor_copy(kscales[:], kscale_pool[:].indirect(offsets[:]))
-        mark_columns(1)
+        mark_columns(0, "q_raw1")
+
+        kwords = sb.tile([P, I], U16, name="kwords", align_bytes=64)
+        nc.vector.tensor_copy(kwords[:], kword_pool[:].indirect(offsets[:]))
+        mark_columns(1, "mark_cols1")
         q_codes = sb.tile([P, 2 * Q], U32, name="q_codes", align_bytes=64)
         q_scales = sb.tile([P, 2 * Q], U8, name="q_scales", align_bytes=64)
         nc.vector.quantize_mx(
             out=q_codes[:].bitcast(FP8X4), scales=q_scales[:], in_=q_grouped[:].rearrange("p w j -> p (w j)")
         )
-        kwords = sb.tile([P, I], U16, name="kwords", align_bytes=64)
+        kscales = sb.tile([P, I], U8, name="kscales", tag="ypool", align_bytes=64)
         points = []
         for h in range(2):
             nc.vector.tensor_copy(
-                kwords[:, h * 256 : (h + 1) * 256], kword_pool[:].indirect(offsets[:, h * 16 : (h + 1) * 16])
+                kscales[:, h * 256 : (h + 1) * 256], kscale_pool[:].indirect(offsets[:, h * 16 : (h + 1) * 16])
             )
             bank = ps.tile([P, 2, 2 * Q], F32, name="points%d" % h)
             for c in range(2):
@@ -123,18 +131,16 @@ def tile_attend_maplace_leaning_readshares_kernel(
                 )
             points.append(bank)
 
-        v_codes = sb.tile([P, E], U32, name="v_codes", align_bytes=64)
-        v_scales = sb.tile([P, E], U8, name="v_scales", align_bytes=64)
         val_picked = []
 
-        def gather_values(j):
-            picked = sb.tile([P, I], BF16, name="val_picked%d" % j, align_bytes=64)
+        def gather_values(j, tag):
+            picked = sb.tile([P, I], BF16, name="val_picked%d" % j, tag=tag, align_bytes=64)
             nc.vector.tensor_copy(picked[:], val_pools[j][:].indirect(offsets[:]))
             val_picked.append(picked)
 
         def quantize_values(j):
             pairs = val_picked[j][:].bitcast(F32)
-            turned = ps2.tile([P, 2, P], F32, name="val_turned")
+            turned = ps.tile([P, 2, P], F32, name="val_turned%d" % j, tag="points%d" % (j % 2))
             for u in range(2):
                 nc.tensor.transpose(turned[:, u, :], pairs[:, u : 2 * P : 2], ident[:])
             grouped = sb.tile([P, P * PACK], BF16, name="val_grouped%d" % j, align_bytes=64)
@@ -147,8 +153,8 @@ def tile_attend_maplace_leaning_readshares_kernel(
                 in_=grouped[:],
             )
 
-        gather_values(0)
-        gather_values(1)
+        gather_values(0, "kscale_pool")
+        gather_values(1, "val_pool0")
 
         dist = ps.tile([P, I], F32, name="dist")
         for r in range(4):
@@ -179,21 +185,21 @@ def tile_attend_maplace_leaning_readshares_kernel(
         )
         ns_flat = ns[:].rearrange("q t s -> q (t s)")
         share = sb.tile([P, I], F32, name="share", align_bytes=64)
-        total = sb.tile([P, 1], F32, name="total")
+        total = sb.tile([P, 1], F32, name="total", align_bytes=64)
         nc.scalar.activation(share[:], ns_flat, ACT.Exp, bias=ns_min[:], scale=-1.0, accum_out=total[:])
         gap = sb.tile([P, I], F32, name="gap", align_bytes=64)
         nc.vector.tensor_scalar(gap[:], ns_flat, ns_min[:], lean_col[:], ALU.subtract, ALU.mult)
-        gather_values(2)
-        inv = sb.tile([P, 1], F32, name="inv")
+        gather_values(2, "lam_col")
+        inv = sb.tile([P, 1], F32, name="inv", tag="val_pool2", align_bytes=64)
         nc.vector.reciprocal(inv[:], total[:])
-        pull = sb.tile([P, I], F32, name="pull", tag="val_pool2", align_bytes=64)
-        mean = sb.tile([P, 1], F32, name="mean")
+        pull = sb.tile([P, I], F32, name="pull", align_bytes=64)
+        mean = sb.tile([P, 1], F32, name="mean", align_bytes=64)
         nc.vector.scalar_tensor_tensor(pull[:], gap[:], inv[:], share[:], ALU.mult, ALU.mult, accum_out=mean[:])
         coef = sb.tile([P, 1], F32, name="coef")
         nc.vector.tensor_scalar(coef[:], mean[:], 1.0, inv[:], ALU.add, ALU.mult)
         w = sb.tile([P, I], F32, name="w", align_bytes=64)
         nc.vector.scalar_tensor_tensor(w[:], share[:], coef[:], pull[:], ALU.mult, ALU.subtract)
-        gather_values(3)
+        gather_values(3, "mean")
         w_turned = ps.tile([P, PACK, Q], F32, name="w_turned", tag="bank_m1")
         for t in range(PACK):
             nc.tensor.transpose(w_turned[:, t, :], w[:, t * P : (t + 1) * P], ident[:])
@@ -210,6 +216,8 @@ def tile_attend_maplace_leaning_readshares_kernel(
             out=w_codes[:].bitcast(FP8X4), scales=w_scales[:], in_=w_grouped[:].rearrange("p q t -> p (q t)")
         )
 
+        v_codes = sb.tile([P, E], U32, name="v_codes", tag="total", align_bytes=64)
+        v_scales = sb.tile([P, E], U8, name="v_scales", align_bytes=64)
         for j in range(4):
             quantize_values(j)
 
@@ -231,6 +239,8 @@ def tile_attend_maplace_leaning_readshares_kernel(
         nc.scalar.activation(oe[:], noz[:], ACT.Exp, bias=noz_min[:], scale=-1.0, accum_out=oe_sum[:])
         oe_inv = sb.tile([P, 1], F32, name="oe_inv")
         nc.vector.reciprocal(oe_inv[:], oe_sum[:])
-        y = sb.tile([P, E], F32, name="y", align_bytes=64)
-        nc.vector.tensor_scalar(y[:], oe[:], oe_inv[:], float(E), ALU.mult, ALU.mult)
-        nc.sync.dma_start(out, y[:])
+        for h, queue in enumerate((nc.sync, nc.scalar)):
+            cols = slice(h * E // 2, (h + 1) * E // 2)
+            y = sb.tile([P, E // 2], F32, name="y%d" % h, align_bytes=64)
+            nc.vector.tensor_scalar(y[:], oe[:, cols], oe_inv[:], float(E), ALU.mult, ALU.mult)
+            queue.dma_start(out[:, cols], y[:])

@@ -44,12 +44,6 @@ def tile_attend_maplace_leaning_readshares_kernel(
             nc.sync.dma_start(val_pool[:], vals[j * P : (j + 1) * P, :])
             return val_pool
 
-        def load_column(name, src):
-            col = sb.tile([P, 1], F32, name=name, align_bytes=64)
-            nc.sync.dma_start(col[:], src)
-            return col
-
-        mark_pools = [load_mark("xpool", xmark)]
         kscale_pool = sb.tile([P, T], U8, name="kscale_pool", align_bytes=64)
         nc.gpsimd.memset(kscale_pool[:].bitcast(I32), 0)
         for quad in range(4):
@@ -57,6 +51,7 @@ def tile_attend_maplace_leaning_readshares_kernel(
                 kscale_pool[32 * quad : 32 * quad + 4, :].bitcast(I32),
                 keys_scales[0, 4 * quad : 4 * quad + 4, :].bitcast(I32),
             )
+        mark_pools = [load_mark("xpool", xmark), load_mark("ypool", ymark)]
         kword_pool = sb.tile([P, T], U16, name="kword_pool", align_bytes=64)
         nc.sync.dma_start(kword_pool[:].bitcast(I32), keys_words[0].bitcast(I32))
         q_raw = []
@@ -64,14 +59,13 @@ def tile_attend_maplace_leaning_readshares_kernel(
             raw = sb.tile([P, PACK, Q], F32, name=name, align_bytes=64)
             nc.sync.dma_start(raw[:], src.rearrange("(p j) w -> p j w", j=PACK))
             q_raw.append(raw)
-        mark_pools.append(load_mark("ypool", ymark))
-        lam_col = load_column("lam_col", lam)
         val_pools = [load_values(0)]
-        lean_col = load_column("lean_col", lean)
+        row_factors = sb.tile([P, Q], F32, name="row_factors", align_bytes=64)
+        for n, src in enumerate((lam, lean, vsharp)):
+            nc.sync.dma_start(row_factors[P - 3 + n : P - 2 + n, :], src.rearrange("q o -> o q"))
+        slot_row = sb.tile([P, I], F32, name="slot_row", align_bytes=64)
+        nc.sync.dma_start(slot_row[MARK_ROW:P, :], slot_factor)
         val_pools.extend([load_values(j) for j in range(1, 4)])
-        os_cols = sb.tile([P, PACK], F32, name="os_cols")
-        nc.sync.dma_start(os_cols[:], slot_factor.rearrange("o (p t) -> (o p) t", t=PACK))
-        vs_col = load_column("vs_col", vsharp)
 
         warm_in = sb.tile([P, 1], F32, name="warm_in")
         nc.gpsimd.memset(warm_in[:], 0.0)
@@ -82,8 +76,8 @@ def tile_attend_maplace_leaning_readshares_kernel(
         nc.gpsimd.memset(mark_pools[0][0:MARK_ROW, 0:X_SPLIT], 0.0)
         nc.vector.memset(mark_pools[0][0:MARK_ROW, X_SPLIT : T + 1], 0.0)
         nc.gpsimd.memset(mark_pools[1][0:MARK_ROW, 0:T], 0.0)
-        nvs_col = sb.tile([P, 1], F32, name="nvs_col")
-        nc.gpsimd.tensor_scalar(nvs_col[:], vs_col[:], -1.0, 0.0, ALU.mult, ALU.add)
+        nc.gpsimd.memset(row_factors[0 : P - 3, :], 0.0)
+        nc.gpsimd.memset(slot_row[0:MARK_ROW, :], 0.0)
 
         mark_cols = []
 
@@ -111,7 +105,7 @@ def tile_attend_maplace_leaning_readshares_kernel(
         nc.vector.quantize_mx(
             out=q_codes[:].bitcast(FP8X4), scales=q_scales[:], in_=q_grouped[:].rearrange("p w j -> p (w j)")
         )
-        kscales = sb.tile([P, I], U8, name="kscales", tag="ypool", align_bytes=64)
+        kscales = sb.tile([P, I], U8, name="kscales", align_bytes=64)
         points = []
         for h in range(2):
             nc.vector.tensor_copy(
@@ -130,6 +124,13 @@ def tile_attend_maplace_leaning_readshares_kernel(
                     stop=True,
                 )
             points.append(bank)
+
+        rows_turned = ps.tile([P, P], F32, name="rows_turned")
+        nc.tensor.transpose(rows_turned[:], row_factors[:], ident[:])
+        lam_lean = sb.tile([P, 2], F32, name="lam_lean")
+        nc.scalar.copy(lam_lean[:], rows_turned[:, P - 3 : P - 1])
+        nvs_col = sb.tile([P, 1], F32, name="nvs_col")
+        nc.scalar.mul(nvs_col[:], rows_turned[:, P - 1 : P], -1.0)
 
         val_picked = []
 
@@ -153,8 +154,8 @@ def tile_attend_maplace_leaning_readshares_kernel(
                 in_=grouped[:],
             )
 
-        gather_values(0, "kscale_pool")
-        gather_values(1, "val_pool0")
+        gather_values(0, "val_picked0")
+        gather_values(1, "val_picked1")
 
         dist = ps.tile([P, I], F32, name="dist")
         for r in range(4):
@@ -178,9 +179,9 @@ def tile_attend_maplace_leaning_readshares_kernel(
                 )
 
         ns = sb.tile([P, PACK, P], F32, name="ns", tag="val_pool1", align_bytes=64)
-        ns_min = sb.tile([P, 1], F32, name="ns_min")
+        ns_min = sb.tile([P, 1], F32, name="ns_min", align_bytes=64)
         nc.vector.tensor_scalar(
-            ns[:], dist[:].rearrange("q (s t) -> q t s", t=PACK), lam_col[:], None, ALU.mult, ALU.min,
+            ns[:], dist[:].rearrange("q (s t) -> q t s", t=PACK), lam_lean[:, 0:1], None, ALU.mult, ALU.min,
             accum_out=ns_min[:],
         )
         ns_flat = ns[:].rearrange("q t s -> q (t s)")
@@ -188,22 +189,27 @@ def tile_attend_maplace_leaning_readshares_kernel(
         total = sb.tile([P, 1], F32, name="total", align_bytes=64)
         nc.scalar.activation(share[:], ns_flat, ACT.Exp, bias=ns_min[:], scale=-1.0, accum_out=total[:])
         gap = sb.tile([P, I], F32, name="gap", align_bytes=64)
-        nc.vector.tensor_scalar(gap[:], ns_flat, ns_min[:], lean_col[:], ALU.subtract, ALU.mult)
-        gather_values(2, "lam_col")
+        nc.gpsimd.tensor_scalar(gap[:], ns_flat, lam_lean[:, 1:2], 0.0, ALU.mult, ALU.add)
+        gather_values(2, "val_picked2")
         inv = sb.tile([P, 1], F32, name="inv", tag="val_pool2", align_bytes=64)
         nc.vector.reciprocal(inv[:], total[:])
         pull = sb.tile([P, I], F32, name="pull", align_bytes=64)
         mean = sb.tile([P, 1], F32, name="mean", align_bytes=64)
         nc.vector.scalar_tensor_tensor(pull[:], gap[:], inv[:], share[:], ALU.mult, ALU.mult, accum_out=mean[:])
-        coef = sb.tile([P, 1], F32, name="coef")
+        gather_values(3, "total")
+        coef = sb.tile([P, 1], F32, name="coef", tag="val_pool3", align_bytes=64)
         nc.vector.tensor_scalar(coef[:], mean[:], 1.0, inv[:], ALU.add, ALU.mult)
         w = sb.tile([P, I], F32, name="w", align_bytes=64)
         nc.vector.scalar_tensor_tensor(w[:], share[:], coef[:], pull[:], ALU.mult, ALU.subtract)
-        gather_values(3, "mean")
+        slots_turned = ps.tile([P, PACK, P], F32, name="slots_turned")
+        for t in range(PACK):
+            nc.tensor.transpose(slots_turned[:, t, :], slot_row[:, t:I:PACK], ident[:])
+        os_cols = sb.tile([P, PACK], F32, name="os_cols", tag="ns_min", align_bytes=64)
+        nc.scalar.copy(os_cols[:], slots_turned[:, :, MARK_ROW])
         w_turned = ps.tile([P, PACK, Q], F32, name="w_turned", tag="bank_m1")
         for t in range(PACK):
             nc.tensor.transpose(w_turned[:, t, :], w[:, t * P : (t + 1) * P], ident[:])
-        w_grouped = sb.tile([P, Q, PACK], BF16, name="w_grouped", tag="val_pool3", align_bytes=64)
+        w_grouped = sb.tile([P, Q, PACK], BF16, name="w_grouped", align_bytes=64)
         nc.vector.tensor_tensor(
             w_grouped[:],
             w_turned[:].rearrange("p t q -> p q t"),
@@ -216,7 +222,7 @@ def tile_attend_maplace_leaning_readshares_kernel(
             out=w_codes[:].bitcast(FP8X4), scales=w_scales[:], in_=w_grouped[:].rearrange("p q t -> p (q t)")
         )
 
-        v_codes = sb.tile([P, E], U32, name="v_codes", tag="total", align_bytes=64)
+        v_codes = sb.tile([P, E], U32, name="v_codes", tag="mean", align_bytes=64)
         v_scales = sb.tile([P, E], U8, name="v_scales", align_bytes=64)
         for j in range(4):
             quantize_values(j)

from contextlib import ExitStack

import concourse.mybir as mybir
from concourse.masks import make_identity

D, T, I, Q, E = 512, 2048, 512, 128, 512
P = 128
PACK = 4
FLOPS = 2 * D * Q * I * 2 + 2 * I * Q * E
BYTES = 2 * D * Q * 4 + P * 2 * T + 16 * T + 2 * T * 4 + 3 * Q * 4 + I * 4 + E * T * 4 + P * 64 + Q * E * 4

F32 = mybir.dt.float32
BF16 = mybir.dt.bfloat16
I32 = mybir.dt.int32
U32 = mybir.dt.uint32
U16 = mybir.dt.uint16
U8 = mybir.dt.uint8
FP8X4 = mybir.dt.float8_e4m3fn_x4
FP4X4 = mybir.dt.float4_e2m1fn_x4
ALU = mybir.AluOpType
ACT = mybir.ActivationFunctionType
MARK_ROW = P - 1
X_SPLIT = 768


def tile_attend_maplace_leaning_readshares_kernel(
    tc, query, query2, keys_words, keys_scales, xmark, ymark, lam, lean, slot_factor, vals, vsharp, offs, out
):
    nc = tc.nc
    with ExitStack() as ctx:
        sb = ctx.enter_context(tc.tile_pool(name="sb", bufs=1))
        ps = ctx.enter_context(tc.psum_pool(name="ps", bufs=1))

        offsets = sb.tile([P, I // 16], U16, name="offsets")
        nc.sync.dma_start(offsets[:], offs)

        def load_mark(name, mark):
            mark_pool = sb.tile([P, T + 1], F32, name=name, align_bytes=64)
            nc.sync.dma_start(mark_pool[MARK_ROW:P, 0:T], mark[MARK_ROW:P, :])
            return mark_pool

        def load_values(j):
            val_pool = sb.tile([P, T], F32, name="val_pool%d" % j, align_bytes=64)
            nc.sync.dma_start(val_pool[:], vals[j * P : (j + 1) * P, :])
            return val_pool

        kscale_pool = sb.tile([P, T], U8, name="kscale_pool", align_bytes=64)
        nc.gpsimd.memset(kscale_pool[:].bitcast(I32), 0)
        for quad in range(4):
            nc.sync.dma_start(
                kscale_pool[32 * quad : 32 * quad + 4, :].bitcast(I32),
                keys_scales[0, 4 * quad : 4 * quad + 4, :].bitcast(I32),
            )
        mark_pools = [load_mark("xpool", xmark), load_mark("ypool", ymark)]
        kword_pool = sb.tile([P, T], U16, name="kword_pool", align_bytes=64)
        nc.sync.dma_start(kword_pool[:].bitcast(I32), keys_words[0].bitcast(I32))
        q_raw = []
        for name, src in (("q_raw0", query), ("q_raw1", query2)):
            raw = sb.tile([P, PACK, Q], F32, name=name, align_bytes=64)
            nc.sync.dma_start(raw[:], src.rearrange("(p j) w -> p j w", j=PACK))
            q_raw.append(raw)
        val_pools = [load_values(0)]
        row_factors = sb.tile([P, Q], F32, name="row_factors", align_bytes=64)
        for n, src in enumerate((lam, lean, vsharp)):
            nc.sync.dma_start(row_factors[P - 3 + n : P - 2 + n, :], src.rearrange("q o -> o q"))
        slot_row = sb.tile([P, I], F32, name="slot_row", align_bytes=64)
        nc.sync.dma_start(slot_row[MARK_ROW:P, :], slot_factor)
        val_pools.extend([load_values(j) for j in range(1, 4)])

        warm_in = sb.tile([P, 1], F32, name="warm_in")
        nc.gpsimd.memset(warm_in[:], 0.0)
        warm = sb.tile([P, 1], F32, name="warm")
        nc.scalar.activation(warm[:], warm_in[:], ACT.Exp)
        ident = sb.tile([P, P], F32, name="ident", align_bytes=64)
        make_identity(nc, ident[:])
        nc.gpsimd.memset(mark_pools[0][0:MARK_ROW, 0:X_SPLIT], 0.0)
        nc.vector.memset(mark_pools[0][0:MARK_ROW, X_SPLIT : T + 1], 0.0)
        nc.gpsimd.memset(mark_pools[1][0:MARK_ROW, 0:T], 0.0)
        nc.gpsimd.memset(row_factors[0 : P - 3, :], 0.0)
        nc.gpsimd.memset(slot_row[0:MARK_ROW, :], 0.0)

        mark_cols = []

        def mark_columns(m, tag):
            picked = sb.tile([P, I], F32, name="mark_picked%d" % m, align_bytes=64)
            nc.vector.tensor_copy(picked[:], mark_pools[m][:, 0:T].indirect(offsets[:]))
            turned = ps.tile([P, 4, P], F32, name="mark_turned%d" % m, tag="bank_m%d" % m)
            for r in range(4):
                nc.tensor.transpose(turned[:, r, :], picked[:, r * P : (r + 1) * P], ident[:])
            cols = sb.tile([P, 4], F32, name="mark_cols%d" % m, tag=tag, align_bytes=64)
            nc.scalar.copy(cols[:], turned[:, :, MARK_ROW])
            mark_cols.append(cols)

        q_grouped = sb.tile([P, 2 * Q, PACK], BF16, name="q_grouped", align_bytes=64)
        for m in range(2):
            nc.scalar.copy(q_grouped[:, m * Q : (m + 1) * Q, :], q_raw[m][:].rearrange("p j w -> p w j"))

        mark_columns(0, "q_raw1")

        kwords = sb.tile([P, I], U16, name="kwords", align_bytes=64)
        nc.vector.tensor_copy(kwords[:], kword_pool[:].indirect(offsets[:]))
        mark_columns(1, "mark_cols1")
        q_codes = sb.tile([P, 2 * Q], U32, name="q_codes", align_bytes=64)
        q_scales = sb.tile([P, 2 * Q], U8, name="q_scales", align_bytes=64)
        nc.vector.quantize_mx(
            out=q_codes[:].bitcast(FP8X4), scales=q_scales[:], in_=q_grouped[:].rearrange("p w j -> p (w j)")
        )
        kscales = sb.tile([P, I], U8, name="kscales", align_bytes=64)
        points = []
        for h in range(2):
            nc.vector.tensor_copy(
                kscales[:, h * 256 : (h + 1) * 256], kscale_pool[:].indirect(offsets[:, h * 16 : (h + 1) * 16])
            )
            bank = ps.tile([P, 2, 2 * Q], F32, name="points%d" % h)
            for c in range(2):
                cols = slice((2 * h + c) * P, (2 * h + c + 1) * P)
                nc.tensor.matmul_mx(
                    out=bank[:, c, :],
                    lhsT=kwords[:, cols].bitcast(FP4X4),
                    lhsT_scale=kscales[:, cols],
                    rhs=q_codes[:].bitcast(FP8X4),
                    rhs_scale=q_scales[:],
                    start=True,
                    stop=True,
                )
            points.append(bank)

        rows_turned = ps.tile([P, P], F32, name="rows_turned")
        nc.tensor.transpose(rows_turned[:], row_factors[:], ident[:])
        lam_lean = sb.tile([P, 2], F32, name="lam_lean")
        nc.scalar.copy(lam_lean[:], rows_turned[:, P - 3 : P - 1])
        nvs_col = sb.tile([P, 1], F32, name="nvs_col")
        nc.scalar.mul(nvs_col[:], rows_turned[:, P - 1 : P], -1.0)

        val_picked = []

        def gather_values(j, tag):
            picked = sb.tile([P, I], BF16, name="val_picked%d" % j, tag=tag, align_bytes=64)
            nc.vector.tensor_copy(picked[:], val_pools[j][:].indirect(offsets[:]))
            val_picked.append(picked)

        def quantize_values(j):
            pairs = val_picked[j][:].bitcast(F32)
            turned = ps.tile([P, 2, P], F32, name="val_turned%d" % j, tag="points%d" % (j % 2))
            for u in range(2):
                nc.tensor.transpose(turned[:, u, :], pairs[:, u : 2 * P : 2], ident[:])
            grouped = sb.tile([P, P * PACK], BF16, name="val_grouped%d" % j, align_bytes=64)
            nc.scalar.copy(
                grouped[:].bitcast(F32).rearrange("p (e u) -> p e u", u=2), turned[:].rearrange("p u e -> p e u")
            )
            nc.vector.quantize_mx(
                out=v_codes[:, j * P : (j + 1) * P].bitcast(FP8X4),
                scales=v_scales[:, j * P : (j + 1) * P],
                in_=grouped[:],
            )

        gather_values(0, "val_picked0")
        gather_values(1, "val_picked1")

        dist = ps.tile([P, I], F32, name="dist")
        for r in range(4):
            sq = sb.tile([P, 2, Q], F32, name="sq%d" % r, align_bytes=64)
            for m in range(2):
                nc.scalar.activation(
                    sq[:, m, :],
                    points[r // 2][:, r % 2, m * Q : (m + 1) * Q],
                    ACT.Square,
                    bias=mark_cols[m][:, r : r + 1],
                    scale=-1.0,
                )
            for m in range(2):
                nc.tensor.matmul(
                    dist[:, r * P : (r + 1) * P],
                    lhsT=sq[:, m, :],
                    rhs=ident[:],
                    is_transpose=True,
                    start=(m == 0),
                    stop=(m == 1),
                )

        ns = sb.tile([P, PACK, P], F32, name="ns", tag="val_pool1", align_bytes=64)
        ns_min = sb.tile([P, 1], F32, name="ns_min", align_bytes=64)
        nc.vector.tensor_scalar(
            ns[:], dist[:].rearrange("q (s t) -> q t s", t=PACK), lam_lean[:, 0:1], None, ALU.mult, ALU.min,
            accum_out=ns_min[:],
        )
        ns_flat = ns[:].rearrange("q t s -> q (t s)")
        share = sb.tile([P, I], F32, name="share", align_bytes=64)
        total = sb.tile([P, 1], F32, name="total", align_bytes=64)
        nc.scalar.activation(share[:], ns_flat, ACT.Exp, bias=ns_min[:], scale=-1.0, accum_out=total[:])
        gap = sb.tile([P, I], F32, name="gap", align_bytes=64)
        nc.gpsimd.tensor_scalar(gap[:], ns_flat, lam_lean[:, 1:2], 0.0, ALU.mult, ALU.add)
        gather_values(2, "val_picked2")
        inv = sb.tile([P, 1], F32, name="inv", tag="val_pool2", align_bytes=64)
        nc.vector.reciprocal(inv[:], total[:])
        pull = sb.tile([P, I], F32, name="pull", align_bytes=64)
        mean = sb.tile([P, 1], F32, name="mean", align_bytes=64)
        nc.vector.scalar_tensor_tensor(pull[:], gap[:], inv[:], share[:], ALU.mult, ALU.mult, accum_out=mean[:])
        gather_values(3, "total")
        coef = sb.tile([P, 1], F32, name="coef", tag="val_pool3", align_bytes=64)
        nc.vector.tensor_scalar(coef[:], mean[:], 1.0, inv[:], ALU.add, ALU.mult)
        w = sb.tile([P, I], F32, name="w", align_bytes=64)
        nc.vector.scalar_tensor_tensor(w[:], share[:], coef[:], pull[:], ALU.mult, ALU.subtract)
        slots_turned = ps.tile([P, PACK, P], F32, name="slots_turned")
        for t in range(PACK):
            nc.tensor.transpose(slots_turned[:, t, :], slot_row[:, t:I:PACK], ident[:])
        os_cols = sb.tile([P, PACK], F32, name="os_cols", tag="ns_min", align_bytes=64)
        nc.scalar.copy(os_cols[:], slots_turned[:, :, MARK_ROW])
        w_turned = ps.tile([P, PACK, Q], F32, name="w_turned", tag="bank_m1")
        for t in range(PACK):
            nc.tensor.transpose(w_turned[:, t, :], w[:, t * P : (t + 1) * P], ident[:])
        w_grouped = sb.tile([P, Q, PACK], BF16, name="w_grouped", align_bytes=64)
        nc.vector.tensor_tensor(
            w_grouped[:],
            w_turned[:].rearrange("p t q -> p q t"),
            os_cols[:].unsqueeze(1).to_broadcast([P, Q, PACK]),
            ALU.mult,
        )
        w_codes = sb.tile([P, Q], U32, name="w_codes", align_bytes=64)
        w_scales = sb.tile([P, Q], U8, name="w_scales", align_bytes=64)
        nc.vector.quantize_mx(
            out=w_codes[:].bitcast(FP8X4), scales=w_scales[:], in_=w_grouped[:].rearrange("p q t -> p (q t)")
        )

        v_codes = sb.tile([P, E], U32, name="v_codes", tag="mean", align_bytes=64)
        v_scales = sb.tile([P, E], U8, name="v_scales", align_bytes=64)
        for j in range(4):
            quantize_values(j)

        o = ps.tile([P, E], F32, name="o", tag="bank_m0")
        nc.tensor.matmul_mx(
            out=o[:],
            lhsT=w_codes[:].bitcast(FP8X4),
            lhsT_scale=w_scales[:],
            rhs=v_codes[:].bitcast(FP8X4),
            rhs_scale=v_scales[:],
            start=True,
            stop=True,
        )
        noz = sb.tile([P, E], F32, name="noz", align_bytes=64)
        noz_min = sb.tile([P, 1], F32, name="noz_min")
        nc.vector.tensor_scalar(noz[:], o[:], nvs_col[:], None, ALU.mult, ALU.min, accum_out=noz_min[:])
        oe = sb.tile([P, E], F32, name="oe", align_bytes=64)
        oe_sum = sb.tile([P, 1], F32, name="oe_sum")
        nc.scalar.activation(oe[:], noz[:], ACT.Exp, bias=noz_min[:], scale=-1.0, accum_out=oe_sum[:])
        oe_inv = sb.tile([P, 1], F32, name="oe_inv")
        nc.vector.reciprocal(oe_inv[:], oe_sum[:])
        for h, queue in enumerate((nc.sync, nc.scalar)):
            cols = slice(h * E // 2, (h + 1) * E // 2)
            y = sb.tile([P, E // 2], F32, name="y%d" % h, align_bytes=64)
            nc.vector.tensor_scalar(y[:], oe[:, cols], oe_inv[:], float(E), ALU.mult, ALU.mult)
            queue.dma_start(out[:, cols], y[:])
